import numpy as np
import ml_dtypes


def mxq(x, axis, fmt="e4m3"):
    dtype, down = {"e4m3": (ml_dtypes.float8_e4m3fn, 7), "e5m2": (ml_dtypes.float8_e5m2, 14)}[fmt]
    v = np.moveaxis(np.asarray(x, np.float32).astype(ml_dtypes.bfloat16).astype(np.float64), axis, -1)
    blocks = v.reshape(v.shape[:-1] + (-1, 32))
    amax = np.abs(blocks).max(-1, keepdims=True)
    byte = np.maximum(np.where(amax > 0, np.frexp(amax)[1] - 1 + 127, 0) - down, 1)
    scale = np.exp2(byte - 127.0)
    codes = (blocks / scale).astype(np.float32).astype(dtype).astype(np.float64)
    return np.moveaxis((codes * scale).reshape(v.shape), -1, axis)


WIDE = False


def mx_kscale(k):
    if not WIDE:
        return np.ones(k)
    levels = np.array([10, -10, 5, -5, 0])
    if k % 512:
        return np.exp2(np.random.permutation(np.resize(levels, k // 32))).repeat(32)
    a = np.empty((k // 512, 16))
    for p in range(k // 512):
        a[p, :8] = np.random.permutation(np.resize(levels, 8))
        for g in range(8):
            far = levels[np.abs(levels - a[p, g]) >= 10]
            a[p, g + 8] = far[np.random.randint(len(far))]
    return np.exp2(a.ravel()).repeat(32)


def f64(x):
    return np.asarray(x).astype(np.float64)


def striped(idx):
    return np.tile(idx.reshape(-1, 16).T, (8, 1)).astype(np.uint16)


def unstriped(offs):
    return offs[:16].T.reshape(-1).astype(np.int64)


def striped8(idx):
    return np.concatenate([x.reshape(-1, 16).T for x in idx]).astype(np.uint16)


def runs(offs, k):
    lists = np.stack([offs[16 * r : 16 * r + 16].T.reshape(-1) for r in range(8)]).astype(np.int64)
    return lists[np.arange(k) % 512 // 64]


def pack_weight(w):
    k, n = w.shape
    w = f64(np.asarray(w, np.float32).astype(ml_dtypes.bfloat16)).reshape(k // 32, 32, n)
    amax = np.abs(w).max(1)
    byte = np.clip(np.where(amax > 0, np.frexp(amax)[1] - 1 + 127 - 7, 1), 1, 254)
    scaled = (w * np.exp2(127.0 - byte)[:, None, :]).reshape(k, n).astype(np.float32)
    words = np.ascontiguousarray(scaled.reshape(k // 512, 128, 4, n).transpose(0, 1, 3, 2)).astype(ml_dtypes.float8_e4m3fn).view(np.uint8)
    return words, np.ascontiguousarray(byte.astype(np.uint8).reshape(k // 512, 16, n))


def unpack_weight(words, scales):
    g, p, n, _ = words.shape
    vals = np.ascontiguousarray(words).view(ml_dtypes.float8_e4m3fn).astype(np.float64) * np.repeat(np.exp2(scales.astype(np.float64) - 127.0), 8, axis=1)[..., None]
    return vals.transpose(0, 1, 3, 2).reshape(g * 512, n)


def sigmoid(v):
    return 1.0 / (1.0 + np.exp(-np.maximum(v, -700.0)))

def planes(y):
    n, m = y.shape
    v = y.astype(np.float32).astype(ml_dtypes.bfloat16).astype(np.float64).reshape(n // 32, 32, m)
    top = np.abs(v).max(1)
    byte = np.clip(np.where(top > 0, np.frexp(top)[1] - 1 + 127 - 7, 1), 1, 254)
    codes = (v * np.exp2(127.0 - byte)[:, None, :]).reshape(n, m).astype(np.float32).astype(ml_dtypes.float8_e4m3fn).view(np.uint8)
    words = codes.reshape(n // 512, 128, 4, m).transpose(0, 1, 3, 2)
    return np.ascontiguousarray(words), np.ascontiguousarray(byte.astype(np.uint8).reshape(n // 512, 16, m))


K, T, S, V, H, W = 512, 2048, 512, 512, 512, 256


def setup_inputs():
    n = np.random.standard_normal
    s = mx_kscale(K)[:, None]
    u = mx_kscale(S)
    packed_xT = pack_weight(n((K, T)) * s)
    packed_w1 = pack_weight(n((K, H)) / np.sqrt(K) / s)
    packed_w2 = pack_weight(n((K, H)) / np.sqrt(K) / s)
    perm = np.stack([np.random.permutation(V) for _ in range(8)])
    return {
        "x_words": packed_xT[0],
        "x_scales": packed_xT[1],
        "w1_words": packed_w1[0],
        "w1_scales": packed_w1[1],
        "w2_words": packed_w2[0],
        "w2_scales": packed_w2[1],
        "ga": (np.random.uniform(0.5, 1.5, (H, 1)) * u[:, None]).astype(np.float32),
        "gb": (np.random.uniform(0.5, 1.5, (H, 1)) / u[:, None]).astype(np.float32),
        "offs": striped(np.random.permutation(T)[:S]),
        "two": striped(np.random.permutation(T)[:V]),
        "n1": striped8(np.stack([np.random.permutation(S) for _ in range(8)])),
        "n2": striped8(perm[:, :W]),
        "n3": striped8(perm[:, W:]),
        "n4": striped8(np.stack([np.random.permutation(V) for _ in range(8)])),
        "n5": striped8(np.stack([np.random.permutation(V) for _ in range(8)])),
    }


def reference(x_words, x_scales, w1_words, w1_scales, w2_words, w2_scales, ga, gb, offs, two, n1, n2, n3, n4, n5):
    xq = unpack_weight(x_words, x_scales)[:, unstriped(offs)]
    a = unpack_weight(w1_words, w1_scales).T @ xq
    z = f64(ga) * (a * (sigmoid(a[np.arange(H)[:, None], runs(n1, H)])))
    x_two = unpack_weight(x_words, x_scales)[:, unstriped(two)]
    b = unpack_weight(w2_words, w2_scales).T @ x_two
    pa = b[np.arange(H)[:, None], runs(n2, H)]
    pb = b[np.arange(H)[:, None], runs(n3, H)]
    rb = pa - pb
    ra = 0.75 * (pa + pb)
    ds = np.zeros((H, V))
    ds[np.arange(H)[:, None], runs(n2, H)] = ra
    dt = ds.copy()
    dt[np.arange(H)[:, None], runs(n3, H)] = rb
    z2 = f64(gb) * dt
    s = 0.0625 * ((mxq(z, 0, "e4m3").T @ mxq(z2, 0, "e4m3")))
    st = s - (s[np.arange(S)[:, None], runs(n4, S)])
    out_0 = st / (np.abs(st[np.arange(S)[:, None], runs(n5, S)]) + 0.5)
    return (out_0,) + planes(out_0)

@@ -1,0 +1,282 @@
+from contextlib import ExitStack
+
+import concourse.mybir as mybir
+
+F32 = mybir.dt.float32
+BF16 = mybir.dt.bfloat16
+I32 = mybir.dt.int32
+U32 = mybir.dt.uint32
+U16 = mybir.dt.uint16
+U8 = mybir.dt.uint8
+FP8X4 = mybir.dt.float8_e4m3fn_x4
+ACT = mybir.ActivationFunctionType
+ALU = mybir.AluOpType
+
+P = 128
+PACK = 4
+T = 2048
+N = 512
+HALF = N // 2
+FLOPS = 3 * 2 * 512 * 512 * 512
+
+
+def tile_picked_kqgatehaarhopn_none_po_kernel(
+    tc, x_words, x_scales, w1_words, w1_scales, w2_words, w2_scales, ga, gb,
+    offs, two, n1, n2, n3, n4, n5, out_0, out_1, out_2,
+):
+    nc = tc.nc
+    with ExitStack() as ctx:
+        lists = ctx.enter_context(tc.tile_pool(name="lists", bufs=1))
+        keep = ctx.enter_context(tc.tile_pool(name="keep", bufs=1))
+        shared = ctx.enter_context(tc.tile_pool(name="shared", bufs=1))
+        psum = ctx.enter_context(tc.psum_pool(name="psum", bufs=1))
+
+        def load_list(src, name):
+            tile = lists.tile(list(src.shape), U16, name=name)
+            nc.sync.dma_start(tile[:], src)
+            return tile
+
+        def load_words(src, width, name):
+            tile = keep.tile([P, width], I32, name=name, align_bytes=64)
+            nc.scalar.dma_start(tile[:], src[0].rearrange("p n t -> p (n t)").bitcast(I32))
+            return tile
+
+        def load_scales(tile, src):
+            for q in range(4):
+                nc.sync.dma_start(tile[32 * q : 32 * q + 4, :].bitcast(I32), src[0, 4 * q : 4 * q + 4, :].bitcast(I32))
+
+        def load_gain(src, name):
+            tile = keep.tile([P, PACK], F32, name=name)
+            nc.sync.dma_start(tile[:], src.rearrange("(p t) o -> p (t o)", t=PACK))
+            return tile
+
+        xs = keep.tile([P, T], U8, name="xs", align_bytes=64)
+        w2s = keep.tile([P, N], U8, name="w2s", align_bytes=64)
+        w1s = keep.tile([P, N], U8, name="w1s", tag="first_pb", align_bytes=64)
+        nc.vector.memset(xs[:].bitcast(I32), 0)
+        nc.vector.memset(w2s[:].bitcast(I32), 0)
+        nc.vector.memset(w1s[:].bitcast(I32), 0)
+
+        xw = load_words(x_words, T, "xw")
+        w2w = load_words(w2_words, N, "w2w")
+        two_t = load_list(two, "two_t")
+        load_scales(xs, x_scales)
+        offs_t = load_list(offs, "offs_t")
+        load_scales(w2s, w2_scales)
+        w1w = load_words(w1_words, N, "w1w")
+        load_scales(w1s, w1_scales)
+        gb_t = load_gain(gb, "gb_t")
+        n3_t = load_list(n3, "n3_t")
+        n2_t = load_list(n2, "n2_t")
+        n1_t = load_list(n1, "n1_t")
+        ga_t = load_gain(ga, "ga_t")
+        n4_t = load_list(n4, "n4_t")
+        n5_t = load_list(n5, "n5_t")
+
+        ones = keep.tile([P, HALF], F32, name="ones")
+        two_thirds = keep.tile([P, HALF], F32, name="two_thirds")
+        nc.gpsimd.memset(ones[:], 1.0)
+        warm = keep.tile([P, 1], F32, name="warm")
+        nc.scalar.activation(warm[:], ones[:, 0:1], ACT.Sigmoid)
+        nc.scalar.activation(two_thirds[:], ones[:], ACT.Copy, scale=2.0 / 3.0)
+        gb15 = keep.tile([P, PACK], F32, name="gb15")
+        nc.scalar.activation(gb15[:], gb_t[:], ACT.Copy, scale=1.5)
+
+        def pick_scales(lst, name):
+            tile = keep.tile([P, N], U8, name=name, align_bytes=64)
+            nc.vector.tensor_copy(tile[:], xs[:].indirect(lst[:]))
+            return tile
+
+        def pick_words(lst, name):
+            tile = keep.tile([P, N], U32, name=name, align_bytes=64)
+            nc.vector.tensor_copy(tile[:], xw[:].bitcast(U32).indirect(lst[:]))
+            return tile
+
+        def deal(src, dtype, name):
+            tile = keep.tile([P, N], dtype, name=name, align_bytes=64)
+            nc.vector.tensor_copy(
+                tile[:].rearrange("p (t m) -> p m t", t=PACK), src[:].rearrange("p (m t) -> p m t", t=PACK)
+            )
+            return tile
+
+        def product(bank, lw, ls, rw, rs, t, cols):
+            m = slice(P * t, P * (t + 1))
+            nc.tensor.matmul_mx(
+                out=bank[:, cols], lhsT=lw[:, m].bitcast(FP8X4), lhsT_scale=ls[:, m],
+                rhs=rw[:, cols].bitcast(FP8X4), rhs_scale=rs[:, cols], start=True, stop=True,
+            )
+
+        whole = slice(0, N)
+        halves = [slice(0, HALF), slice(HALF, N)]
+        list_halves = [slice(0, 16), slice(16, 32)]
+
+        two_s = pick_scales(two_t, "two_s")
+        offs_s = pick_scales(offs_t, "offs_s")
+        w2w_d = deal(w2w, I32, "w2w_d")
+        w2s_d = deal(w2s, U8, "w2s_d")
+        two_w = pick_words(two_t, "two_w")
+
+        b_sb = []
+        for t in range(PACK):
+            bank = psum.tile([P, N], F32, name=f"b_ps{t}", tag=f"left{t}")
+            product(bank, w2w_d, w2s_d, two_w, two_s, t, whole)
+            tile = keep.tile([P, N], F32, name=f"b_sb{t}")
+            nc.scalar.activation(tile[:], bank[:], ACT.Copy, scale=gb15[:, t : t + 1])
+            b_sb.append(tile)
+
+        offs_w = pick_words(offs_t, "offs_w")
+        w1w_d = deal(w1w, I32, "w1w_d")
+        w1s_d = deal(w1s, U8, "w1s_d")
+        a_ps = []
+        for t in range(PACK):
+            bank = psum.tile([P, N], F32, name=f"a_ps{t}", tag=f"right{t}")
+            product(bank, w1w_d, w1s_d, offs_w, offs_s, t, whole)
+            a_ps.append(bank)
+
+        z_rows = keep.tile([P, PACK, N], BF16, name="z_rows")
+        z_in = keep.tile([P, N * PACK], BF16, name="z_in", align_bytes=64)
+        z2_in = [keep.tile([P, HALF, PACK], BF16, name=f"z2_in{h}", align_bytes=64) for h in range(2)]
+
+        pbs, diffs = [], []
+        for t in range(PACK):
+            pb = keep.tile([P, HALF], F32, name=f"pb{t}", tag="first_pb" if t == 0 else f"pb{t}", align_bytes=64)
+            nc.vector.tensor_copy(pb[:], b_sb[t][:].indirect(n3_t[:]))
+            diff = keep.tile([P, HALF], F32, name=f"diff{t}")
+            nc.vector.tensor_tensor(diff[:], b_sb[t][:].indirect(n2_t[:]), pb[:], ALU.subtract)
+            pbs.append(pb)
+            diffs.append(diff)
+
+        a_sb = []
+        for t in range(PACK):
+            tile = keep.tile([P, N], F32, name=f"a_sb{t}")
+            nc.scalar.copy(tile[:], a_ps[t][:])
+            a_sb.append(tile)
+        half_diffs = []
+        for t in range(PACK):
+            tile = keep.tile([P, HALF], F32, name=f"half_diff{t}")
+            nc.scalar.activation(tile[:], diffs[t][:], ACT.Copy, scale=0.5)
+            half_diffs.append(tile)
+
+        row_bytes = 4 * N
+        sigs = []
+        for t in range(PACK):
+            if t == PACK - 1:
+                sig = shared.tile([P, N], F32, name=f"sig{t}", offset=row_bytes // 2)
+            else:
+                sig = keep.tile([P, N], F32, name=f"sig{t}")
+            for h in range(2):
+                nc.scalar.activation(sig[:, halves[h]], a_sb[t][:].indirect(n1_t[:, list_halves[h]]), ACT.Sigmoid)
+            sigs.append(sig)
+
+        def scatter_pair(ts, dts):
+            for t, dt in zip(ts, dts):
+                nc.vector.tensor_tensor(dt[:].indirect(n3_t[:]), diffs[t][:], two_thirds[:], ALU.mult)
+            for t, dt in zip(ts, dts):
+                nc.vector.tensor_tensor(dt[:].indirect(n2_t[:]), pbs[t][:], half_diffs[t][:], ALU.add)
+
+        def regroup(t, dt):
+            for h in range(2):
+                nc.scalar.copy(z2_in[h][:, :, t], dt[:, halves[h]])
+
+        early = [keep.tile([P, N], F32, name=f"dt{t}") for t in range(2)]
+        scatter_pair((0, 1), early)
+        for t in range(PACK):
+            nc.vector.scalar_tensor_tensor(
+                z_rows[:, t, :], a_ps[t][:], ga_t[:, t : t + 1], sigs[t][:], ALU.mult, ALU.mult
+            )
+        late = [shared.tile([P, N], F32, name=f"dt{2 + i}", offset=i * row_bytes) for i in range(2)]
+        scatter_pair((2, 3), late)
+        regroup(0, early[0])
+        regroup(1, early[1])
+        src = z_rows[:].rearrange("p t (a b u) -> p a u b t", b=2, u=PACK)
+        dst = z_in[:].rearrange("p (u a b t) -> p a u b t", u=PACK, b=2, t=PACK)
+        nc.scalar.copy(dst, src)
+        warm2 = keep.tile([P, 1], F32, name="warm2")
+        nc.scalar.activation(warm2[:], z_in[:, 0:1], ACT.Abs_reciprocal_sqrt, bias=1.0, scale=0.0)
+        regroup(2, late[0])
+        regroup(3, late[1])
+
+        z_w = keep.tile([P, N], U32, name="z_w", align_bytes=64)
+        z_s = keep.tile([P, N], U8, name="z_s", align_bytes=64)
+        nc.vector.quantize_mx(out=z_w[:].bitcast(FP8X4), scales=z_s[:], in_=z_in[:])
+        z2_w = keep.tile([P, N], U32, name="z2_w", align_bytes=64)
+        z2_s = keep.tile([P, N], U8, name="z2_s", align_bytes=64)
+        for h in range(2):
+            nc.vector.quantize_mx(
+                out=z2_w[:, halves[h]].bitcast(FP8X4), scales=z2_s[:, halves[h]],
+                in_=z2_in[h][:].rearrange("p c t -> p (c t)"),
+            )
+
+        s_ps = [psum.tile([P, N], F32, name=f"s_ps{t}", tag=f"left{t}") for t in range(PACK)]
+        for t in range(PACK):
+            for h in range(2):
+                product(s_ps[t], z_w, z_s, z2_w, z2_s, t, halves[h])
+
+        result = [keep.tile([P, PACK, HALF], F32, name=f"result{h}") for h in range(2)]
+        out_rows = out_0.rearrange("(p t) v -> p t v", t=PACK)
+
+        def row_tiles(name):
+            return [keep.tile([P, N], F32, name=f"{name}{t}") for t in range(PACK)]
+
+        s_neg, s_pos, st = row_tiles("s_neg"), row_tiles("s_pos"), row_tiles("st")
+        size, root, inverse = row_tiles("size"), row_tiles("root"), row_tiles("inverse")
+
+        def leave_neg(t):
+            nc.scalar.activation(s_neg[t][:], s_ps[t][:], ACT.Copy, scale=-0.0625)
+
+        def leave_pos(t):
+            if t >= 2:
+                nc.scalar.activation(s_pos[t][:], s_ps[t][:], ACT.Copy, scale=0.0625)
+            else:
+                nc.vector.tensor_scalar(s_pos[t][:], s_ps[t][:], 0.0625, None, ALU.mult)
+            for h in range(2):
+                nc.vector.tensor_tensor(
+                    st[t][:, halves[h]], s_neg[t][:].indirect(n4_t[:, list_halves[h]]), s_pos[t][:, halves[h]], ALU.add
+                )
+
+        def take_size(t):
+            nc.scalar.activation(size[t][:], st[t][:], ACT.Abs)
+
+        def take_root(t):
+            nc.scalar.activation(root[t][:], size[t][:], ACT.Abs_reciprocal_sqrt, bias=0.5)
+
+        def finish(t):
+            nc.scalar.activation(inverse[t][:], root[t][:], ACT.Square)
+            for h in range(2):
+                nc.vector.tensor_tensor(
+                    result[h][:, t, :], inverse[t][:].indirect(n5_t[:, list_halves[h]]), st[t][:, halves[h]], ALU.mult
+                )
+                nc.sync.dma_start(out_rows[:, t, halves[h]], result[h][:, t, :])
+
+        leave_neg(0)
+        leave_pos(0)
+        leave_neg(1)
+        leave_pos(1)
+        leave_neg(2)
+        leave_pos(2)
+        leave_neg(3)
+        take_size(0)
+        leave_pos(3)
+        for t in range(PACK):
+            take_root(t)
+            if t + 1 < PACK:
+                take_size(t + 1)
+            finish(t)
+
+        o_w = keep.tile([P, N], I32, name="o_w", align_bytes=64)
+        o_s = keep.tile([P, N], U8, name="o_s", align_bytes=64)
+        words_out = out_1[0].rearrange("p n t -> p (n t)").bitcast(I32)
+        for h in range(2):
+            o_in = keep.tile([P, HALF, PACK], BF16, name=f"o_in{h}", align_bytes=64)
+            engine_copy = nc.scalar.copy if h == 0 else nc.vector.tensor_copy
+            engine_copy(
+                o_in[:].rearrange("p (c i) t -> p c t i", i=4), result[h][:].rearrange("p t (c i) -> p c t i", i=4)
+            )
+            nc.vector.quantize_mx(
+                out=o_w[:, halves[h]].bitcast(FP8X4), scales=o_s[:, halves[h]],
+                in_=o_in[:].rearrange("p c t -> p (c t)"),
+            )
+            nc.sync.dma_start(words_out[:, halves[h]], o_w[:, halves[h]])
+        for q in range(4):
+            queue = nc.sync if q % 2 == 0 else nc.scalar
+            queue.dma_start(out_2[0, 4 * q : 4 * q + 4, :].bitcast(I32), o_s[32 * q : 32 * q + 4, :].bitcast(I32))

@@ -36,14 +36,17 @@ def tile_picked_kqgatehaarhopn_none_po_kernel(
             nc.sync.dma_start(tile[:], src)
             return tile
 
-        def load_words(src, width, name):
+        def load_words(src, width, name, queue):
             tile = keep.tile([P, width], I32, name=name, align_bytes=64)
-            nc.scalar.dma_start(tile[:], src[0].rearrange("p n t -> p (n t)").bitcast(I32))
+            queue.dma_start(tile[:], src[0].rearrange("p n t -> p (n t)").bitcast(I32))
             return tile
 
         def load_scales(tile, src):
             for q in range(4):
-                nc.sync.dma_start(tile[32 * q : 32 * q + 4, :].bitcast(I32), src[0, 4 * q : 4 * q + 4, :].bitcast(I32))
+                rows = src[0, 4 * q : 4 * q + 4, :].bitcast(I32)
+                nc.sync.dma_start(
+                    tile[32 * q : 32 * q + 32, :].bitcast(I32), rows.unsqueeze(0).broadcast_to([8] + list(rows.shape))
+                )
 
         def load_gain(src, name):
             tile = keep.tile([P, PACK], F32, name=name)
@@ -53,19 +56,19 @@ def tile_picked_kqgatehaarhopn_none_po_kernel(
         xs = keep.tile([P, T], U8, name="xs", align_bytes=64)
         w2s = keep.tile([P, N], U8, name="w2s", align_bytes=64)
         w1s = keep.tile([P, N], U8, name="w1s", tag="first_pb", align_bytes=64)
-        nc.vector.memset(xs[:].bitcast(I32), 0)
-        nc.vector.memset(w2s[:].bitcast(I32), 0)
-        nc.vector.memset(w1s[:].bitcast(I32), 0)
-
-        xw = load_words(x_words, T, "xw")
-        w2w = load_words(w2_words, N, "w2w")
-        two_t = load_list(two, "two_t")
+        seed = keep.tile([P, 1], F32, name="seed")
+        nc.gpsimd.memset(seed[:], 0.0)
+        warm = keep.tile([P, 1], F32, name="warm")
+        nc.scalar.activation(warm[:], seed[:], ACT.Sigmoid)
         load_scales(xs, x_scales)
+        two_t = load_list(two, "two_t")
         offs_t = load_list(offs, "offs_t")
+        w2w = load_words(w2_words, N, "w2w", nc.sync)
+        xw = load_words(x_words, T, "xw", nc.sync)
         load_scales(w2s, w2_scales)
-        w1w = load_words(w1_words, N, "w1w")
-        load_scales(w1s, w1_scales)
         gb_t = load_gain(gb, "gb_t")
+        w1w = load_words(w1_words, N, "w1w", nc.sync)
+        load_scales(w1s, w1_scales)
         n3_t = load_list(n3, "n3_t")
         n2_t = load_list(n2, "n2_t")
         n1_t = load_list(n1, "n1_t")
@@ -75,9 +78,7 @@ def tile_picked_kqgatehaarhopn_none_po_kernel(
 
         ones = keep.tile([P, HALF], F32, name="ones")
         two_thirds = keep.tile([P, HALF], F32, name="two_thirds")
-        nc.gpsimd.memset(ones[:], 1.0)
-        warm = keep.tile([P, 1], F32, name="warm")
-        nc.scalar.activation(warm[:], ones[:, 0:1], ACT.Sigmoid)
+        nc.vector.memset(ones[:], 1.0)
         nc.scalar.activation(two_thirds[:], ones[:], ACT.Copy, scale=2.0 / 3.0)
         gb15 = keep.tile([P, PACK], F32, name="gb15")
         nc.scalar.activation(gb15[:], gb_t[:], ACT.Copy, scale=1.5)
@@ -94,8 +95,10 @@ def tile_picked_kqgatehaarhopn_none_po_kernel(
 
         def deal(src, dtype, name):
             tile = keep.tile([P, N], dtype, name=name, align_bytes=64)
+            run = 4 if dtype == I32 else 16
             nc.vector.tensor_copy(
-                tile[:].rearrange("p (t m) -> p m t", t=PACK), src[:].rearrange("p (m t) -> p m t", t=PACK)
+                tile[:].rearrange("p (t c i) -> p c t i", t=PACK, i=run),
+                src[:].rearrange("p (c i t) -> p c t i", t=PACK, i=run),
             )
             return tile
 
@@ -135,7 +138,7 @@ def tile_picked_kqgatehaarhopn_none_po_kernel(
 
         z_rows = keep.tile([P, PACK, N], BF16, name="z_rows")
         z_in = keep.tile([P, N * PACK], BF16, name="z_in", align_bytes=64)
-        z2_in = [keep.tile([P, HALF, PACK], BF16, name=f"z2_in{h}", align_bytes=64) for h in range(2)]
+        z2_pairs = [keep.tile([P, 2, HALF, 2], BF16, name=f"z2_pairs{h}") for h in range(2)]
 
         pbs, diffs = [], []
         for t in range(PACK):
@@ -167,6 +170,8 @@ def tile_picked_kqgatehaarhopn_none_po_kernel(
             for h in range(2):
                 nc.scalar.activation(sig[:, halves[h]], a_sb[t][:].indirect(n1_t[:, list_halves[h]]), ACT.Sigmoid)
             sigs.append(sig)
+        warm2 = keep.tile([P, 1], F32, name="warm2")
+        nc.scalar.activation(warm2[:], sigs[-1][:, N - 1 : N], ACT.Abs_reciprocal_sqrt, bias=0.5)
 
         def scatter_pair(ts, dts):
             for t, dt in zip(ts, dts):
@@ -176,7 +181,7 @@ def tile_picked_kqgatehaarhopn_none_po_kernel(
 
         def regroup(t, dt):
             for h in range(2):
-                nc.scalar.copy(z2_in[h][:, :, t], dt[:, halves[h]])
+                nc.scalar.copy(z2_pairs[h][:, t // 2, :, t % 2], dt[:, halves[h]])
 
         early = [keep.tile([P, N], F32, name=f"dt{t}") for t in range(2)]
         scatter_pair((0, 1), early)
@@ -191,8 +196,6 @@ def tile_picked_kqgatehaarhopn_none_po_kernel(
         src = z_rows[:].rearrange("p t (a b u) -> p a u b t", b=2, u=PACK)
         dst = z_in[:].rearrange("p (u a b t) -> p a u b t", u=PACK, b=2, t=PACK)
         nc.scalar.copy(dst, src)
-        warm2 = keep.tile([P, 1], F32, name="warm2")
-        nc.scalar.activation(warm2[:], z_in[:, 0:1], ACT.Abs_reciprocal_sqrt, bias=1.0, scale=0.0)
         regroup(2, late[0])
         regroup(3, late[1])
 
@@ -202,10 +205,12 @@ def tile_picked_kqgatehaarhopn_none_po_kernel(
         z2_w = keep.tile([P, N], U32, name="z2_w", align_bytes=64)
         z2_s = keep.tile([P, N], U8, name="z2_s", align_bytes=64)
         for h in range(2):
-            nc.vector.quantize_mx(
-                out=z2_w[:, halves[h]].bitcast(FP8X4), scales=z2_s[:, halves[h]],
-                in_=z2_in[h][:].rearrange("p c t -> p (c t)"),
+            z2_in = keep.tile([P, HALF * PACK], BF16, name=f"z2_in{h}", align_bytes=64)
+            nc.vector.tensor_copy(
+                z2_in[:].bitcast(F32).rearrange("p (c u) -> p c u", u=2),
+                z2_pairs[h][:].rearrange("p u c e -> p (u c e)").bitcast(F32).rearrange("p (u c) -> p c u", u=2),
             )
+            nc.vector.quantize_mx(out=z2_w[:, halves[h]].bitcast(FP8X4), scales=z2_s[:, halves[h]], in_=z2_in[:])
 
         s_ps = [psum.tile([P, N], F32, name=f"s_ps{t}", tag=f"left{t}") for t in range(PACK)]
         for t in range(PACK):
@@ -226,12 +231,14 @@ def tile_picked_kqgatehaarhopn_none_po_kernel(
 
         def leave_pos(t):
             if t >= 2:
-                nc.scalar.activation(s_pos[t][:], s_ps[t][:], ACT.Copy, scale=0.0625)
+                nc.sync.dma_start(s_pos[t][:], s_neg[t][:])
+            elif t == 1:
+                nc.vector.tensor_scalar(s_pos[t][:], s_ps[t][:], -0.0625, None, ALU.mult)
             else:
-                nc.vector.tensor_scalar(s_pos[t][:], s_ps[t][:], 0.0625, None, ALU.mult)
+                nc.scalar.activation(s_pos[t][:], s_ps[t][:], ACT.Copy, scale=-0.0625)
             for h in range(2):
                 nc.vector.tensor_tensor(
-                    st[t][:, halves[h]], s_neg[t][:].indirect(n4_t[:, list_halves[h]]), s_pos[t][:, halves[h]], ALU.add
+                    st[t][:, halves[h]], s_neg[t][:].indirect(n4_t[:, list_halves[h]]), s_pos[t][:, halves[h]], ALU.subtract
                 )
 
         def take_size(t):
@@ -250,13 +257,11 @@ def tile_picked_kqgatehaarhopn_none_po_kernel(
 
         leave_neg(0)
         leave_pos(0)
-        leave_neg(1)
-        leave_pos(1)
-        leave_neg(2)
-        leave_pos(2)
-        leave_neg(3)
+        for t in (2, 1, 3):
+            leave_neg(t)
+        for t in range(1, PACK):
+            leave_pos(t)
         take_size(0)
-        leave_pos(3)
         for t in range(PACK):
             take_root(t)
             if t + 1 < PACK:

@@ -17,6 +17,8 @@ PACK = 4
 T = 2048
 N = 512
 HALF = N // 2
+ROW = 4 * N
+PB_AT = 4 * ROW
 FLOPS = 3 * 2 * 512 * 512 * 512
 
 
@@ -41,34 +43,34 @@ def tile_picked_kqgatehaarhopn_none_po_kernel(
             queue.dma_start(tile[:], src[0].rearrange("p n t -> p (n t)").bitcast(I32))
             return tile
 
-        def load_scales(tile, src):
+        def load_scales(tile, src, queue):
             for q in range(4):
                 rows = src[0, 4 * q : 4 * q + 4, :].bitcast(I32)
-                nc.sync.dma_start(
+                queue.dma_start(
                     tile[32 * q : 32 * q + 32, :].bitcast(I32), rows.unsqueeze(0).broadcast_to([8] + list(rows.shape))
                 )
 
         def load_gain(src, name):
             tile = keep.tile([P, PACK], F32, name=name)
-            nc.sync.dma_start(tile[:], src.rearrange("(p t) o -> p (t o)", t=PACK))
+            nc.gpsimd.dma_start(tile[:], src.rearrange("(p t) o -> p (t o)", t=PACK))
             return tile
 
         xs = keep.tile([P, T], U8, name="xs", align_bytes=64)
-        w2s = keep.tile([P, N], U8, name="w2s", align_bytes=64)
-        w1s = keep.tile([P, N], U8, name="w1s", tag="first_pb", align_bytes=64)
+        w2s = keep.tile([P, N], U8, name="w2s", tag="offs_w", align_bytes=64)
+        w1s = shared.tile([P, N], U8, name="w1s", offset=PB_AT, align_bytes=64)
         seed = keep.tile([P, 1], F32, name="seed")
         nc.gpsimd.memset(seed[:], 0.0)
         warm = keep.tile([P, 1], F32, name="warm")
         nc.scalar.activation(warm[:], seed[:], ACT.Sigmoid)
-        load_scales(xs, x_scales)
+        load_scales(xs, x_scales, nc.sync)
         two_t = load_list(two, "two_t")
         offs_t = load_list(offs, "offs_t")
         w2w = load_words(w2_words, N, "w2w", nc.sync)
         xw = load_words(x_words, T, "xw", nc.sync)
-        load_scales(w2s, w2_scales)
+        load_scales(w2s, w2_scales, nc.sync)
         gb_t = load_gain(gb, "gb_t")
         w1w = load_words(w1_words, N, "w1w", nc.sync)
-        load_scales(w1s, w1_scales)
+        load_scales(w1s, w1_scales, nc.gpsimd)
         n3_t = load_list(n3, "n3_t")
         n2_t = load_list(n2, "n2_t")
         n1_t = load_list(n1, "n1_t")
@@ -80,8 +82,11 @@ def tile_picked_kqgatehaarhopn_none_po_kernel(
         two_thirds = keep.tile([P, HALF], F32, name="two_thirds")
         nc.vector.memset(ones[:], 1.0)
         nc.scalar.activation(two_thirds[:], ones[:], ACT.Copy, scale=2.0 / 3.0)
-        gb15 = keep.tile([P, PACK], F32, name="gb15")
-        nc.scalar.activation(gb15[:], gb_t[:], ACT.Copy, scale=1.5)
+        gb15 = []
+        for u in range(2):
+            tile = shared.tile([P, 2], F32, name=f"gb15_{u}", offset=PB_AT + u * ROW // 2 + N)
+            nc.scalar.activation(tile[:], gb_t[:, 2 * u : 2 * u + 2], ACT.Copy, scale=1.5)
+            gb15.append(tile)
 
         def pick_scales(lst, name):
             tile = keep.tile([P, N], U8, name=name, align_bytes=64)
@@ -123,8 +128,11 @@ def tile_picked_kqgatehaarhopn_none_po_kernel(
         for t in range(PACK):
             bank = psum.tile([P, N], F32, name=f"b_ps{t}", tag=f"left{t}")
             product(bank, w2w_d, w2s_d, two_w, two_s, t, whole)
-            tile = keep.tile([P, N], F32, name=f"b_sb{t}")
-            nc.scalar.activation(tile[:], bank[:], ACT.Copy, scale=gb15[:, t : t + 1])
+            if t == 2:
+                tile = shared.tile([P, N], F32, name=f"b_sb{t}", offset=ROW // 2)
+            else:
+                tile = keep.tile([P, N], F32, name=f"b_sb{t}")
+            nc.scalar.activation(tile[:], bank[:], ACT.Copy, scale=gb15[t // 2][:, t % 2 : t % 2 + 1])
             b_sb.append(tile)
 
         offs_w = pick_words(offs_t, "offs_w")
@@ -141,35 +149,42 @@ def tile_picked_kqgatehaarhopn_none_po_kernel(
         z2_pairs = [keep.tile([P, 2, HALF, 2], BF16, name=f"z2_pairs{h}") for h in range(2)]
 
         pbs, diffs = [], []
-        for t in range(PACK):
-            pb = keep.tile([P, HALF], F32, name=f"pb{t}", tag="first_pb" if t == 0 else f"pb{t}", align_bytes=64)
-            nc.vector.tensor_copy(pb[:], b_sb[t][:].indirect(n3_t[:]))
-            diff = keep.tile([P, HALF], F32, name=f"diff{t}")
-            nc.vector.tensor_tensor(diff[:], b_sb[t][:].indirect(n2_t[:]), pb[:], ALU.subtract)
-            pbs.append(pb)
-            diffs.append(diff)
+        for u in range(2):
+            for t in (2 * u, 2 * u + 1):
+                if t % 2 == 0:
+                    pb = shared.tile([P, HALF], F32, name=f"pb{t}", offset=PB_AT + u * ROW // 2)
+                else:
+                    pb = keep.tile([P, HALF], F32, name=f"pb{t}")
+                nc.vector.tensor_copy(pb[:], b_sb[t][:].indirect(n3_t[:]))
+                pbs.append(pb)
+            for t in (2 * u, 2 * u + 1):
+                diff = keep.tile([P, HALF], F32, name=f"diff{t}")
+                nc.vector.tensor_tensor(diff[:], b_sb[t][:].indirect(n2_t[:]), pbs[t][:], ALU.subtract)
+                diffs.append(diff)
 
         a_sb = []
         for t in range(PACK):
             tile = keep.tile([P, N], F32, name=f"a_sb{t}")
             nc.scalar.copy(tile[:], a_ps[t][:])
             a_sb.append(tile)
-        half_diffs = []
-        for t in range(PACK):
-            tile = keep.tile([P, HALF], F32, name=f"half_diff{t}")
-            nc.scalar.activation(tile[:], diffs[t][:], ACT.Copy, scale=0.5)
-            half_diffs.append(tile)
+        half_diffs = [keep.tile([P, HALF], F32, name=f"half_diff{t}") for t in range(PACK)]
 
-        row_bytes = 4 * N
+        def halve(t):
+            nc.scalar.activation(half_diffs[t][:], diffs[t][:], ACT.Copy, scale=0.5)
+
+        halve(0)
+        halve(1)
         sigs = []
         for t in range(PACK):
             if t == PACK - 1:
-                sig = shared.tile([P, N], F32, name=f"sig{t}", offset=row_bytes // 2)
+                sig = shared.tile([P, N], F32, name=f"sig{t}", offset=2 * ROW + ROW // 2)
             else:
                 sig = keep.tile([P, N], F32, name=f"sig{t}")
             for h in range(2):
                 nc.scalar.activation(sig[:, halves[h]], a_sb[t][:].indirect(n1_t[:, list_halves[h]]), ACT.Sigmoid)
             sigs.append(sig)
+        halve(2)
+        halve(3)
         warm2 = keep.tile([P, 1], F32, name="warm2")
         nc.scalar.activation(warm2[:], sigs[-1][:, N - 1 : N], ACT.Abs_reciprocal_sqrt, bias=0.5)
 
@@ -183,13 +198,13 @@ def tile_picked_kqgatehaarhopn_none_po_kernel(
             for h in range(2):
                 nc.scalar.copy(z2_pairs[h][:, t // 2, :, t % 2], dt[:, halves[h]])
 
-        early = [keep.tile([P, N], F32, name=f"dt{t}") for t in range(2)]
+        early = [shared.tile([P, N], F32, name=f"dt{t}", offset=t * ROW) for t in range(2)]
         scatter_pair((0, 1), early)
         for t in range(PACK):
             nc.vector.scalar_tensor_tensor(
                 z_rows[:, t, :], a_ps[t][:], ga_t[:, t : t + 1], sigs[t][:], ALU.mult, ALU.mult
             )
-        late = [shared.tile([P, N], F32, name=f"dt{2 + i}", offset=i * row_bytes) for i in range(2)]
+        late = [shared.tile([P, N], F32, name=f"dt{2 + i}", offset=(2 + i) * ROW) for i in range(2)]
         scatter_pair((2, 3), late)
         regroup(0, early[0])
         regroup(1, early[1])
@@ -213,7 +228,7 @@ def tile_picked_kqgatehaarhopn_none_po_kernel(
             nc.vector.quantize_mx(out=z2_w[:, halves[h]].bitcast(FP8X4), scales=z2_s[:, halves[h]], in_=z2_in[:])
 
         s_ps = [psum.tile([P, N], F32, name=f"s_ps{t}", tag=f"left{t}") for t in range(PACK)]
-        for t in range(PACK):
+        for t in (0, 1, 3, 2):
             for h in range(2):
                 product(s_ps[t], z_w, z_s, z2_w, z2_s, t, halves[h])
 
@@ -230,9 +245,9 @@ def tile_picked_kqgatehaarhopn_none_po_kernel(
             nc.scalar.activation(s_neg[t][:], s_ps[t][:], ACT.Copy, scale=-0.0625)
 
         def leave_pos(t):
-            if t >= 2:
+            if t == 3:
                 nc.sync.dma_start(s_pos[t][:], s_neg[t][:])
-            elif t == 1:
+            elif t < 2:
                 nc.vector.tensor_scalar(s_pos[t][:], s_ps[t][:], -0.0625, None, ALU.mult)
             else:
                 nc.scalar.activation(s_pos[t][:], s_ps[t][:], ACT.Copy, scale=-0.0625)
@@ -257,7 +272,7 @@ def tile_picked_kqgatehaarhopn_none_po_kernel(
 
         leave_neg(0)
         leave_pos(0)
-        for t in (2, 1, 3):
+        for t in (1, 3, 2):
             leave_neg(t)
         for t in range(1, PACK):
             leave_pos(t)

@@ -14,12 +14,17 @@ ALU = mybir.AluOpType
 
 P = 128
 PACK = 4
-T = 2048
+QUADRANT = 32
+TOKENS = 2048
 N = 512
 HALF = N // 2
+LINE = 16
 ROW = 4 * N
-PB_AT = 4 * ROW
-FLOPS = 3 * 2 * 512 * 512 * 512
+FLOPS = 3 * 2 * N * N * N
+
+EARLY_DT = 0
+LATE_DT = 2 * ROW
+PB = 4 * ROW
 
 
 def tile_picked_kqgatehaarhopn_none_po_kernel(
@@ -27,6 +32,10 @@ def tile_picked_kqgatehaarhopn_none_po_kernel(
     offs, two, n1, n2, n3, n4, n5, out_0, out_1, out_2,
 ):
     nc = tc.nc
+    whole = slice(0, N)
+    halves = [slice(0, HALF), slice(HALF, N)]
+    list_halves = [slice(0, HALF // 16), slice(HALF // 16, N // 16)]
+
     with ExitStack() as ctx:
         lists = ctx.enter_context(tc.tile_pool(name="lists", bufs=1))
         keep = ctx.enter_context(tc.tile_pool(name="keep", bufs=1))
@@ -38,16 +47,17 @@ def tile_picked_kqgatehaarhopn_none_po_kernel(
             nc.sync.dma_start(tile[:], src)
             return tile
 
-        def load_words(src, width, name, queue):
+        def load_words(src, width, name):
             tile = keep.tile([P, width], I32, name=name, align_bytes=64)
-            queue.dma_start(tile[:], src[0].rearrange("p n t -> p (n t)").bitcast(I32))
+            nc.sync.dma_start(tile[:], src[0].rearrange("p n t -> p (n t)").bitcast(I32))
             return tile
 
-        def load_scales(tile, src, queue):
-            for q in range(4):
+        def load_scales(tile, src):
+            for q in range(P // QUADRANT):
                 rows = src[0, 4 * q : 4 * q + 4, :].bitcast(I32)
-                queue.dma_start(
-                    tile[32 * q : 32 * q + 32, :].bitcast(I32), rows.unsqueeze(0).broadcast_to([8] + list(rows.shape))
+                nc.sync.dma_start(
+                    tile[QUADRANT * q : QUADRANT * (q + 1), :].bitcast(I32),
+                    rows.unsqueeze(0).broadcast_to([QUADRANT // 4] + list(rows.shape)),
                 )
 
         def load_gain(src, name):
@@ -55,22 +65,23 @@ def tile_picked_kqgatehaarhopn_none_po_kernel(
             nc.gpsimd.dma_start(tile[:], src.rearrange("(p t) o -> p (t o)", t=PACK))
             return tile
 
-        xs = keep.tile([P, T], U8, name="xs", align_bytes=64)
-        w2s = keep.tile([P, N], U8, name="w2s", tag="offs_w", align_bytes=64)
-        w1s = shared.tile([P, N], U8, name="w1s", offset=PB_AT, align_bytes=64)
-        seed = keep.tile([P, 1], F32, name="seed")
-        nc.gpsimd.memset(seed[:], 0.0)
-        warm = keep.tile([P, 1], F32, name="warm")
-        nc.scalar.activation(warm[:], seed[:], ACT.Sigmoid)
-        load_scales(xs, x_scales, nc.sync)
+        zero = keep.tile([P, 1], F32, name="zero")
+        nc.gpsimd.memset(zero[:], 0.0)
+        one_half = keep.tile([P, 1], F32, name="one_half")
+        nc.scalar.activation(one_half[:], zero[:], ACT.Sigmoid)
+
+        x_s = keep.tile([P, TOKENS], U8, name="x_s", align_bytes=64)
+        w2_s = keep.tile([P, N], U8, name="w2_s", tag="offs_w", align_bytes=64)
+        w1_s = shared.tile([P, N], U8, name="w1_s", offset=PB, align_bytes=64)
+        load_scales(x_s, x_scales)
         two_t = load_list(two, "two_t")
         offs_t = load_list(offs, "offs_t")
-        w2w = load_words(w2_words, N, "w2w", nc.sync)
-        xw = load_words(x_words, T, "xw", nc.sync)
-        load_scales(w2s, w2_scales, nc.sync)
+        w2_w = load_words(w2_words, N, "w2_w")
+        x_w = load_words(x_words, TOKENS, "x_w")
+        load_scales(w2_s, w2_scales)
         gb_t = load_gain(gb, "gb_t")
-        w1w = load_words(w1_words, N, "w1w", nc.sync)
-        load_scales(w1s, w1_scales, nc.gpsimd)
+        w1_w = load_words(w1_words, N, "w1_w")
+        load_scales(w1_s, w1_scales)
         n3_t = load_list(n3, "n3_t")
         n2_t = load_list(n2, "n2_t")
         n1_t = load_list(n1, "n1_t")
@@ -79,105 +90,98 @@ def tile_picked_kqgatehaarhopn_none_po_kernel(
         n5_t = load_list(n5, "n5_t")
 
         ones = keep.tile([P, HALF], F32, name="ones")
-        two_thirds = keep.tile([P, HALF], F32, name="two_thirds")
         nc.vector.memset(ones[:], 1.0)
+        two_thirds = keep.tile([P, HALF], F32, name="two_thirds")
         nc.scalar.activation(two_thirds[:], ones[:], ACT.Copy, scale=2.0 / 3.0)
-        gb15 = []
+        gb_scaled = []
         for u in range(2):
-            tile = shared.tile([P, 2], F32, name=f"gb15_{u}", offset=PB_AT + u * ROW // 2 + N)
+            tile = shared.tile([P, 2], F32, name=f"gb_scaled{u}", offset=PB + u * ROW // 2 + N)
             nc.scalar.activation(tile[:], gb_t[:, 2 * u : 2 * u + 2], ACT.Copy, scale=1.5)
-            gb15.append(tile)
+            gb_scaled.append(tile)
 
-        def pick_scales(lst, name):
+        def pick_scales(offsets, name):
             tile = keep.tile([P, N], U8, name=name, align_bytes=64)
-            nc.vector.tensor_copy(tile[:], xs[:].indirect(lst[:]))
+            nc.vector.tensor_copy(tile[:], x_s[:].indirect(offsets[:]))
             return tile
 
-        def pick_words(lst, name):
+        def pick_words(offsets, name):
             tile = keep.tile([P, N], U32, name=name, align_bytes=64)
-            nc.vector.tensor_copy(tile[:], xw[:].bitcast(U32).indirect(lst[:]))
+            nc.vector.tensor_copy(tile[:], x_w[:].bitcast(U32).indirect(offsets[:]))
             return tile
 
-        def deal(src, dtype, name):
+        def deal(src, dtype, itemsize, name):
             tile = keep.tile([P, N], dtype, name=name, align_bytes=64)
-            run = 4 if dtype == I32 else 16
             nc.vector.tensor_copy(
-                tile[:].rearrange("p (t c i) -> p c t i", t=PACK, i=run),
-                src[:].rearrange("p (c i t) -> p c t i", t=PACK, i=run),
+                tile[:].rearrange("p (t c i) -> p c t i", t=PACK, i=LINE // itemsize),
+                src[:].rearrange("p (c i t) -> p c t i", t=PACK, i=LINE // itemsize),
             )
             return tile
 
-        def product(bank, lw, ls, rw, rs, t, cols):
+        def product(bank, left_w, left_s, right_w, right_s, t, cols):
             m = slice(P * t, P * (t + 1))
             nc.tensor.matmul_mx(
-                out=bank[:, cols], lhsT=lw[:, m].bitcast(FP8X4), lhsT_scale=ls[:, m],
-                rhs=rw[:, cols].bitcast(FP8X4), rhs_scale=rs[:, cols], start=True, stop=True,
+                out=bank[:, cols], lhsT=left_w[:, m].bitcast(FP8X4), lhsT_scale=left_s[:, m],
+                rhs=right_w[:, cols].bitcast(FP8X4), rhs_scale=right_s[:, cols], start=True, stop=True,
             )
 
-        whole = slice(0, N)
-        halves = [slice(0, HALF), slice(HALF, N)]
-        list_halves = [slice(0, 16), slice(16, 32)]
+        def row_tiles(name, width):
+            return [keep.tile([P, width], F32, name=f"{name}{t}") for t in range(PACK)]
 
         two_s = pick_scales(two_t, "two_s")
         offs_s = pick_scales(offs_t, "offs_s")
-        w2w_d = deal(w2w, I32, "w2w_d")
-        w2s_d = deal(w2s, U8, "w2s_d")
+        w2_wd = deal(w2_w, I32, 4, "w2_wd")
+        w2_sd = deal(w2_s, U8, 1, "w2_sd")
         two_w = pick_words(two_t, "two_w")
 
         b_sb = []
         for t in range(PACK):
             bank = psum.tile([P, N], F32, name=f"b_ps{t}", tag=f"left{t}")
-            product(bank, w2w_d, w2s_d, two_w, two_s, t, whole)
+            product(bank, w2_wd, w2_sd, two_w, two_s, t, whole)
             if t == 2:
-                tile = shared.tile([P, N], F32, name=f"b_sb{t}", offset=ROW // 2)
+                tile = shared.tile([P, N], F32, name=f"b_sb{t}", offset=EARLY_DT + ROW // 2)
             else:
                 tile = keep.tile([P, N], F32, name=f"b_sb{t}")
-            nc.scalar.activation(tile[:], bank[:], ACT.Copy, scale=gb15[t // 2][:, t % 2 : t % 2 + 1])
+            nc.scalar.activation(tile[:], bank[:], ACT.Copy, scale=gb_scaled[t // 2][:, t % 2 : t % 2 + 1])
             b_sb.append(tile)
 
         offs_w = pick_words(offs_t, "offs_w")
-        w1w_d = deal(w1w, I32, "w1w_d")
-        w1s_d = deal(w1s, U8, "w1s_d")
+        w1_wd = deal(w1_w, I32, 4, "w1_wd")
+        w1_sd = deal(w1_s, U8, 1, "w1_sd")
         a_ps = []
         for t in range(PACK):
             bank = psum.tile([P, N], F32, name=f"a_ps{t}", tag=f"right{t}")
-            product(bank, w1w_d, w1s_d, offs_w, offs_s, t, whole)
+            product(bank, w1_wd, w1_sd, offs_w, offs_s, t, whole)
             a_ps.append(bank)
-
-        z_rows = keep.tile([P, PACK, N], BF16, name="z_rows")
-        z_in = keep.tile([P, N * PACK], BF16, name="z_in", align_bytes=64)
-        z2_pairs = [keep.tile([P, 2, HALF, 2], BF16, name=f"z2_pairs{h}") for h in range(2)]
 
         pbs, diffs = [], []
         for u in range(2):
-            for t in (2 * u, 2 * u + 1):
-                if t % 2 == 0:
-                    pb = shared.tile([P, HALF], F32, name=f"pb{t}", offset=PB_AT + u * ROW // 2)
+            pair = (2 * u, 2 * u + 1)
+            for t in pair:
+                if t == pair[0]:
+                    pb = shared.tile([P, HALF], F32, name=f"pb{t}", offset=PB + u * ROW // 2)
                 else:
                     pb = keep.tile([P, HALF], F32, name=f"pb{t}")
                 nc.vector.tensor_copy(pb[:], b_sb[t][:].indirect(n3_t[:]))
                 pbs.append(pb)
-            for t in (2 * u, 2 * u + 1):
+            for t in pair:
                 diff = keep.tile([P, HALF], F32, name=f"diff{t}")
                 nc.vector.tensor_tensor(diff[:], b_sb[t][:].indirect(n2_t[:]), pbs[t][:], ALU.subtract)
                 diffs.append(diff)
 
-        a_sb = []
+        a_sb = row_tiles("a_sb", N)
         for t in range(PACK):
-            tile = keep.tile([P, N], F32, name=f"a_sb{t}")
-            nc.scalar.copy(tile[:], a_ps[t][:])
-            a_sb.append(tile)
-        half_diffs = [keep.tile([P, HALF], F32, name=f"half_diff{t}") for t in range(PACK)]
+            nc.scalar.copy(a_sb[t][:], a_ps[t][:])
+        half_diffs = row_tiles("half_diff", HALF)
 
         def halve(t):
-            nc.scalar.activation(half_diffs[t][:], diffs[t][:], ACT.Copy, scale=0.5)
+            nc.scalar.activation(half_diffs[t][:], diffs[t][:], ACT.Copy, scale=one_half[:])
 
         halve(0)
         halve(1)
         sigs = []
         for t in range(PACK):
             if t == PACK - 1:
-                sig = shared.tile([P, N], F32, name=f"sig{t}", offset=2 * ROW + ROW // 2)
+                sig = shared.tile([P, N], F32, name=f"sig{t}", offset=LATE_DT + ROW // 2)
             else:
                 sig = keep.tile([P, N], F32, name=f"sig{t}")
             for h in range(2):
@@ -185,8 +189,8 @@ def tile_picked_kqgatehaarhopn_none_po_kernel(
             sigs.append(sig)
         halve(2)
         halve(3)
-        warm2 = keep.tile([P, 1], F32, name="warm2")
-        nc.scalar.activation(warm2[:], sigs[-1][:, N - 1 : N], ACT.Abs_reciprocal_sqrt, bias=0.5)
+        warm = keep.tile([P, 1], F32, name="warm")
+        nc.scalar.activation(warm[:], sigs[-1][:, N - 1 : N], ACT.Abs_reciprocal_sqrt, bias=0.5)
 
         def scatter_pair(ts, dts):
             for t, dt in zip(ts, dts):
@@ -194,25 +198,31 @@ def tile_picked_kqgatehaarhopn_none_po_kernel(
             for t, dt in zip(ts, dts):
                 nc.vector.tensor_tensor(dt[:].indirect(n2_t[:]), pbs[t][:], half_diffs[t][:], ALU.add)
 
-        def regroup(t, dt):
-            for h in range(2):
-                nc.scalar.copy(z2_pairs[h][:, t // 2, :, t % 2], dt[:, halves[h]])
-
-        early = [shared.tile([P, N], F32, name=f"dt{t}", offset=t * ROW) for t in range(2)]
+        early = [shared.tile([P, N], F32, name=f"dt{i}", offset=EARLY_DT + i * ROW) for i in range(2)]
         scatter_pair((0, 1), early)
+        z_rows = keep.tile([P, PACK, N], BF16, name="z_rows")
         for t in range(PACK):
             nc.vector.scalar_tensor_tensor(
                 z_rows[:, t, :], a_ps[t][:], ga_t[:, t : t + 1], sigs[t][:], ALU.mult, ALU.mult
             )
-        late = [shared.tile([P, N], F32, name=f"dt{2 + i}", offset=(2 + i) * ROW) for i in range(2)]
+        late = [shared.tile([P, N], F32, name=f"dt{2 + i}", offset=LATE_DT + i * ROW) for i in range(2)]
         scatter_pair((2, 3), late)
-        regroup(0, early[0])
-        regroup(1, early[1])
-        src = z_rows[:].rearrange("p t (a b u) -> p a u b t", b=2, u=PACK)
-        dst = z_in[:].rearrange("p (u a b t) -> p a u b t", u=PACK, b=2, t=PACK)
-        nc.scalar.copy(dst, src)
-        regroup(2, late[0])
-        regroup(3, late[1])
+
+        z2_pairs = [keep.tile([P, 2, HALF, 2], BF16, name=f"z2_pairs{h}") for h in range(2)]
+
+        def round_z2(t, dt):
+            for h in range(2):
+                nc.scalar.copy(z2_pairs[h][:, t // 2, :, t % 2], dt[:, halves[h]])
+
+        round_z2(0, early[0])
+        round_z2(1, early[1])
+        z_in = keep.tile([P, N * PACK], BF16, name="z_in", align_bytes=64)
+        nc.scalar.copy(
+            z_in[:].rearrange("p (u c e t) -> p c u e t", u=PACK, e=2, t=PACK),
+            z_rows[:].rearrange("p t (c e u) -> p c u e t", e=2, u=PACK),
+        )
+        round_z2(2, late[0])
+        round_z2(3, late[1])
 
         z_w = keep.tile([P, N], U32, name="z_w", align_bytes=64)
         z_s = keep.tile([P, N], U8, name="z_s", align_bytes=64)
@@ -228,32 +238,28 @@ def tile_picked_kqgatehaarhopn_none_po_kernel(
             nc.vector.quantize_mx(out=z2_w[:, halves[h]].bitcast(FP8X4), scales=z2_s[:, halves[h]], in_=z2_in[:])
 
         s_ps = [psum.tile([P, N], F32, name=f"s_ps{t}", tag=f"left{t}") for t in range(PACK)]
-        for t in (0, 1, 3, 2):
-            for h in range(2):
-                product(s_ps[t], z_w, z_s, z2_w, z2_s, t, halves[h])
+        s_first = psum.tile([P, N], F32, name="s_first", tag="right0")
+        product(s_first, z_w, z_s, z2_w, z2_s, 0, halves[0])
+        product(s_ps[0], z_w, z_s, z2_w, z2_s, 0, halves[1])
+        for t in (1, 3, 2):
+            product(s_ps[t], z_w, z_s, z2_w, z2_s, t, whole)
 
+        s_window, s_plain, st = row_tiles("s_window", N), row_tiles("s_plain", N), row_tiles("st", N)
+        size, root, inverse = row_tiles("size", N), row_tiles("root", N), row_tiles("inverse", N)
         result = [keep.tile([P, PACK, HALF], F32, name=f"result{h}") for h in range(2)]
         out_rows = out_0.rearrange("(p t) v -> p t v", t=PACK)
 
-        def row_tiles(name):
-            return [keep.tile([P, N], F32, name=f"{name}{t}") for t in range(PACK)]
+        def leave_by_scalar(dst, bank, cols):
+            nc.scalar.activation(dst[:, cols], bank[:, cols], ACT.Copy, scale=-0.0625)
 
-        s_neg, s_pos, st = row_tiles("s_neg"), row_tiles("s_pos"), row_tiles("st")
-        size, root, inverse = row_tiles("size"), row_tiles("root"), row_tiles("inverse")
+        def leave_by_vector(dst, bank, cols):
+            nc.vector.tensor_scalar(dst[:, cols], bank[:, cols], -0.0625, None, ALU.mult)
 
-        def leave_neg(t):
-            nc.scalar.activation(s_neg[t][:], s_ps[t][:], ACT.Copy, scale=-0.0625)
-
-        def leave_pos(t):
-            if t == 3:
-                nc.sync.dma_start(s_pos[t][:], s_neg[t][:])
-            elif t < 2:
-                nc.vector.tensor_scalar(s_pos[t][:], s_ps[t][:], -0.0625, None, ALU.mult)
-            else:
-                nc.scalar.activation(s_pos[t][:], s_ps[t][:], ACT.Copy, scale=-0.0625)
+        def centre(t):
             for h in range(2):
                 nc.vector.tensor_tensor(
-                    st[t][:, halves[h]], s_neg[t][:].indirect(n4_t[:, list_halves[h]]), s_pos[t][:, halves[h]], ALU.subtract
+                    st[t][:, halves[h]], s_window[t][:].indirect(n4_t[:, list_halves[h]]),
+                    s_plain[t][:, halves[h]], ALU.subtract,
                 )
 
         def take_size(t):
@@ -270,33 +276,43 @@ def tile_picked_kqgatehaarhopn_none_po_kernel(
                 )
                 nc.sync.dma_start(out_rows[:, t, halves[h]], result[h][:, t, :])
 
-        leave_neg(0)
-        leave_pos(0)
-        for t in (1, 3, 2):
-            leave_neg(t)
-        for t in range(1, PACK):
-            leave_pos(t)
+        for bank, cols in ((s_first, halves[0]), (s_ps[0], halves[1])):
+            leave_by_scalar(s_window[0], bank, cols)
+            leave_by_scalar(s_plain[0], bank, cols)
+        centre(0)
+        leave_by_scalar(s_window[1], s_ps[1], whole)
+        leave_by_vector(s_plain[1], s_ps[1], whole)
+        centre(1)
+        leave_by_scalar(s_window[3], s_ps[3], whole)
+        nc.sync.dma_start(s_plain[3][:], s_window[3][:])
+        leave_by_scalar(s_window[2], s_ps[2], whole)
         take_size(0)
+        leave_by_scalar(s_plain[2], s_ps[2], halves[0])
+        leave_by_vector(s_plain[2], s_ps[2], halves[1])
+        centre(2)
+        centre(3)
         for t in range(PACK):
             take_root(t)
             if t + 1 < PACK:
                 take_size(t + 1)
             finish(t)
 
-        o_w = keep.tile([P, N], I32, name="o_w", align_bytes=64)
-        o_s = keep.tile([P, N], U8, name="o_s", align_bytes=64)
+        out_w = keep.tile([P, N], I32, name="out_w", align_bytes=64)
+        out_s = keep.tile([P, N], U8, name="out_s", align_bytes=64)
         words_out = out_1[0].rearrange("p n t -> p (n t)").bitcast(I32)
-        for h in range(2):
-            o_in = keep.tile([P, HALF, PACK], BF16, name=f"o_in{h}", align_bytes=64)
-            engine_copy = nc.scalar.copy if h == 0 else nc.vector.tensor_copy
-            engine_copy(
-                o_in[:].rearrange("p (c i) t -> p c t i", i=4), result[h][:].rearrange("p t (c i) -> p c t i", i=4)
+        for h, regroup in enumerate((nc.scalar.copy, nc.vector.tensor_copy)):
+            out_in = keep.tile([P, HALF, PACK], BF16, name=f"out_in{h}", align_bytes=64)
+            regroup(
+                out_in[:].rearrange("p (c i) t -> p c t i", i=LINE // 4),
+                result[h][:].rearrange("p t (c i) -> p c t i", i=LINE // 4),
             )
             nc.vector.quantize_mx(
-                out=o_w[:, halves[h]].bitcast(FP8X4), scales=o_s[:, halves[h]],
-                in_=o_in[:].rearrange("p c t -> p (c t)"),
+                out=out_w[:, halves[h]].bitcast(FP8X4), scales=out_s[:, halves[h]],
+                in_=out_in[:].rearrange("p c t -> p (c t)"),
             )
-            nc.sync.dma_start(words_out[:, halves[h]], o_w[:, halves[h]])
-        for q in range(4):
+            nc.sync.dma_start(words_out[:, halves[h]], out_w[:, halves[h]])
+        for q in range(P // QUADRANT):
             queue = nc.sync if q % 2 == 0 else nc.scalar
-            queue.dma_start(out_2[0, 4 * q : 4 * q + 4, :].bitcast(I32), o_s[32 * q : 32 * q + 4, :].bitcast(I32))
+            queue.dma_start(
+                out_2[0, 4 * q : 4 * q + 4, :].bitcast(I32), out_s[QUADRANT * q : QUADRANT * q + 4, :].bitcast(I32)
+            )

from contextlib import ExitStack

import concourse.mybir as mybir

F32 = mybir.dt.float32
BF16 = mybir.dt.bfloat16
I32 = mybir.dt.int32
U32 = mybir.dt.uint32
U16 = mybir.dt.uint16
U8 = mybir.dt.uint8
FP8X4 = mybir.dt.float8_e4m3fn_x4
ACT = mybir.ActivationFunctionType
ALU = mybir.AluOpType

P = 128
PACK = 4
QUADRANT = 32
TOKENS = 2048
N = 512
HALF = N // 2
LINE = 16
ROW = 4 * N
FLOPS = 3 * 2 * N * N * N

EARLY_DT = 0
LATE_DT = 2 * ROW
PB = 4 * ROW


def tile_picked_kqgatehaarhopn_none_po_kernel(
    tc, x_words, x_scales, w1_words, w1_scales, w2_words, w2_scales, ga, gb,
    offs, two, n1, n2, n3, n4, n5, out_0, out_1, out_2,
):
    nc = tc.nc
    whole = slice(0, N)
    halves = [slice(0, HALF), slice(HALF, N)]
    list_halves = [slice(0, HALF // 16), slice(HALF // 16, N // 16)]

    with ExitStack() as ctx:
        lists = ctx.enter_context(tc.tile_pool(name="lists", bufs=1))
        keep = ctx.enter_context(tc.tile_pool(name="keep", bufs=1))
        shared = ctx.enter_context(tc.tile_pool(name="shared", bufs=1))
        psum = ctx.enter_context(tc.psum_pool(name="psum", bufs=1))

        def load_list(src, name):
            tile = lists.tile(list(src.shape), U16, name=name)
            nc.sync.dma_start(tile[:], src)
            return tile

        def load_words(src, width, name):
            tile = keep.tile([P, width], I32, name=name, align_bytes=64)
            nc.sync.dma_start(tile[:], src[0].rearrange("p n t -> p (n t)").bitcast(I32))
            return tile

        def load_scales(tile, src):
            for q in range(P // QUADRANT):
                rows = src[0, 4 * q : 4 * q + 4, :].bitcast(I32)
                nc.sync.dma_start(
                    tile[QUADRANT * q : QUADRANT * (q + 1), :].bitcast(I32),
                    rows.unsqueeze(0).broadcast_to([QUADRANT // 4] + list(rows.shape)),
                )

        def load_gain(src, name):
            tile = keep.tile([P, PACK], F32, name=name)
            nc.gpsimd.dma_start(tile[:], src.rearrange("(p t) o -> p (t o)", t=PACK))
            return tile

        zero = keep.tile([P, 1], F32, name="zero")
        nc.gpsimd.memset(zero[:], 0.0)
        one_half = keep.tile([P, 1], F32, name="one_half")
        nc.scalar.activation(one_half[:], zero[:], ACT.Sigmoid)

        x_s = keep.tile([P, TOKENS], U8, name="x_s", align_bytes=64)
        w2_s = keep.tile([P, N], U8, name="w2_s", tag="offs_w", align_bytes=64)
        w1_s = shared.tile([P, N], U8, name="w1_s", offset=PB, align_bytes=64)
        load_scales(x_s, x_scales)
        two_t = load_list(two, "two_t")
        offs_t = load_list(offs, "offs_t")
        w2_w = load_words(w2_words, N, "w2_w")
        x_w = load_words(x_words, TOKENS, "x_w")
        load_scales(w2_s, w2_scales)
        gb_t = load_gain(gb, "gb_t")
        w1_w = load_words(w1_words, N, "w1_w")
        load_scales(w1_s, w1_scales)
        n3_t = load_list(n3, "n3_t")
        n2_t = load_list(n2, "n2_t")
        n1_t = load_list(n1, "n1_t")
        ga_t = load_gain(ga, "ga_t")
        n4_t = load_list(n4, "n4_t")
        n5_t = load_list(n5, "n5_t")

        ones = keep.tile([P, HALF], F32, name="ones")
        nc.vector.memset(ones[:], 1.0)
        two_thirds = keep.tile([P, HALF], F32, name="two_thirds")
        nc.scalar.activation(two_thirds[:], ones[:], ACT.Copy, scale=2.0 / 3.0)
        gb_scaled = []
        for u in range(2):
            tile = shared.tile([P, 2], F32, name=f"gb_scaled{u}", offset=PB + u * ROW // 2 + N)
            nc.scalar.activation(tile[:], gb_t[:, 2 * u : 2 * u + 2], ACT.Copy, scale=1.5)
            gb_scaled.append(tile)

        def pick_scales(offsets, name):
            tile = keep.tile([P, N], U8, name=name, align_bytes=64)
            nc.vector.tensor_copy(tile[:], x_s[:].indirect(offsets[:]))
            return tile

        def pick_words(offsets, name):
            tile = keep.tile([P, N], U32, name=name, align_bytes=64)
            nc.vector.tensor_copy(tile[:], x_w[:].bitcast(U32).indirect(offsets[:]))
            return tile

        def deal(src, dtype, itemsize, name):
            tile = keep.tile([P, N], dtype, name=name, align_bytes=64)
            nc.vector.tensor_copy(
                tile[:].rearrange("p (t c i) -> p c t i", t=PACK, i=LINE // itemsize),
                src[:].rearrange("p (c i t) -> p c t i", t=PACK, i=LINE // itemsize),
            )
            return tile

        def product(bank, left_w, left_s, right_w, right_s, t, cols):
            m = slice(P * t, P * (t + 1))
            nc.tensor.matmul_mx(
                out=bank[:, cols], lhsT=left_w[:, m].bitcast(FP8X4), lhsT_scale=left_s[:, m],
                rhs=right_w[:, cols].bitcast(FP8X4), rhs_scale=right_s[:, cols], start=True, stop=True,
            )

        def row_tiles(name, width):
            return [keep.tile([P, width], F32, name=f"{name}{t}") for t in range(PACK)]

        two_s = pick_scales(two_t, "two_s")
        offs_s = pick_scales(offs_t, "offs_s")
        w2_wd = deal(w2_w, I32, 4, "w2_wd")
        w2_sd = deal(w2_s, U8, 1, "w2_sd")
        two_w = pick_words(two_t, "two_w")

        b_sb = []
        for t in range(PACK):
            bank = psum.tile([P, N], F32, name=f"b_ps{t}", tag=f"left{t}")
            product(bank, w2_wd, w2_sd, two_w, two_s, t, whole)
            if t == 2:
                tile = shared.tile([P, N], F32, name=f"b_sb{t}", offset=EARLY_DT + ROW // 2)
            else:
                tile = keep.tile([P, N], F32, name=f"b_sb{t}")
            nc.scalar.activation(tile[:], bank[:], ACT.Copy, scale=gb_scaled[t // 2][:, t % 2 : t % 2 + 1])
            b_sb.append(tile)

        offs_w = pick_words(offs_t, "offs_w")
        w1_wd = deal(w1_w, I32, 4, "w1_wd")
        w1_sd = deal(w1_s, U8, 1, "w1_sd")
        a_ps = []
        for t in range(PACK):
            bank = psum.tile([P, N], F32, name=f"a_ps{t}", tag=f"right{t}")
            product(bank, w1_wd, w1_sd, offs_w, offs_s, t, whole)
            a_ps.append(bank)

        pbs, diffs = [], []
        for u in range(2):
            pair = (2 * u, 2 * u + 1)
            for t in pair:
                if t == pair[0]:
                    pb = shared.tile([P, HALF], F32, name=f"pb{t}", offset=PB + u * ROW // 2)
                else:
                    pb = keep.tile([P, HALF], F32, name=f"pb{t}")
                nc.vector.tensor_copy(pb[:], b_sb[t][:].indirect(n3_t[:]))
                pbs.append(pb)
            for t in pair:
                diff = keep.tile([P, HALF], F32, name=f"diff{t}")
                nc.vector.tensor_tensor(diff[:], b_sb[t][:].indirect(n2_t[:]), pbs[t][:], ALU.subtract)
                diffs.append(diff)

        a_sb = row_tiles("a_sb", N)
        for t in range(PACK):
            nc.scalar.copy(a_sb[t][:], a_ps[t][:])
        half_diffs = row_tiles("half_diff", HALF)

        def halve(t):
            nc.scalar.activation(half_diffs[t][:], diffs[t][:], ACT.Copy, scale=one_half[:])

        halve(0)
        halve(1)
        sigs = []
        for t in range(PACK):
            if t == PACK - 1:
                sig = shared.tile([P, N], F32, name=f"sig{t}", offset=LATE_DT + ROW // 2)
            else:
                sig = keep.tile([P, N], F32, name=f"sig{t}")
            for h in range(2):
                nc.scalar.activation(sig[:, halves[h]], a_sb[t][:].indirect(n1_t[:, list_halves[h]]), ACT.Sigmoid)
            sigs.append(sig)
        halve(2)
        halve(3)
        warm = keep.tile([P, 1], F32, name="warm")
        nc.scalar.activation(warm[:], sigs[-1][:, N - 1 : N], ACT.Abs_reciprocal_sqrt, bias=0.5)

        def scatter_pair(ts, dts):
            for t, dt in zip(ts, dts):
                nc.vector.tensor_tensor(dt[:].indirect(n3_t[:]), diffs[t][:], two_thirds[:], ALU.mult)
            for t, dt in zip(ts, dts):
                nc.vector.tensor_tensor(dt[:].indirect(n2_t[:]), pbs[t][:], half_diffs[t][:], ALU.add)

        early = [shared.tile([P, N], F32, name=f"dt{i}", offset=EARLY_DT + i * ROW) for i in range(2)]
        scatter_pair((0, 1), early)
        z_rows = keep.tile([P, PACK, N], BF16, name="z_rows")
        for t in range(PACK):
            nc.vector.scalar_tensor_tensor(
                z_rows[:, t, :], a_ps[t][:], ga_t[:, t : t + 1], sigs[t][:], ALU.mult, ALU.mult
            )
        late = [shared.tile([P, N], F32, name=f"dt{2 + i}", offset=LATE_DT + i * ROW) for i in range(2)]
        scatter_pair((2, 3), late)

        z2_pairs = [keep.tile([P, 2, HALF, 2], BF16, name=f"z2_pairs{h}") for h in range(2)]

        def round_z2(t, dt):
            for h in range(2):
                nc.scalar.copy(z2_pairs[h][:, t // 2, :, t % 2], dt[:, halves[h]])

        round_z2(0, early[0])
        round_z2(1, early[1])
        z_in = keep.tile([P, N * PACK], BF16, name="z_in", align_bytes=64)
        nc.scalar.copy(
            z_in[:].rearrange("p (u c e t) -> p c u e t", u=PACK, e=2, t=PACK),
            z_rows[:].rearrange("p t (c e u) -> p c u e t", e=2, u=PACK),
        )
        round_z2(2, late[0])
        round_z2(3, late[1])

        z_w = keep.tile([P, N], U32, name="z_w", align_bytes=64)
        z_s = keep.tile([P, N], U8, name="z_s", align_bytes=64)
        nc.vector.quantize_mx(out=z_w[:].bitcast(FP8X4), scales=z_s[:], in_=z_in[:])
        z2_w = keep.tile([P, N], U32, name="z2_w", align_bytes=64)
        z2_s = keep.tile([P, N], U8, name="z2_s", align_bytes=64)
        for h in range(2):
            z2_in = keep.tile([P, HALF * PACK], BF16, name=f"z2_in{h}", align_bytes=64)
            nc.vector.tensor_copy(
                z2_in[:].bitcast(F32).rearrange("p (c u) -> p c u", u=2),
                z2_pairs[h][:].rearrange("p u c e -> p (u c e)").bitcast(F32).rearrange("p (u c) -> p c u", u=2),
            )
            nc.vector.quantize_mx(out=z2_w[:, halves[h]].bitcast(FP8X4), scales=z2_s[:, halves[h]], in_=z2_in[:])

        s_ps = [psum.tile([P, N], F32, name=f"s_ps{t}", tag=f"left{t}") for t in range(PACK)]
        s_first = psum.tile([P, N], F32, name="s_first", tag="right0")
        product(s_first, z_w, z_s, z2_w, z2_s, 0, halves[0])
        product(s_ps[0], z_w, z_s, z2_w, z2_s, 0, halves[1])
        for t in (1, 3, 2):
            product(s_ps[t], z_w, z_s, z2_w, z2_s, t, whole)

        s_window, s_plain, st = row_tiles("s_window", N), row_tiles("s_plain", N), row_tiles("st", N)
        size, root, inverse = row_tiles("size", N), row_tiles("root", N), row_tiles("inverse", N)
        result = [keep.tile([P, PACK, HALF], F32, name=f"result{h}") for h in range(2)]
        out_rows = out_0.rearrange("(p t) v -> p t v", t=PACK)

        def leave_by_scalar(dst, bank, cols):
            nc.scalar.activation(dst[:, cols], bank[:, cols], ACT.Copy, scale=-0.0625)

        def leave_by_vector(dst, bank, cols):
            nc.vector.tensor_scalar(dst[:, cols], bank[:, cols], -0.0625, None, ALU.mult)

        def centre(t):
            for h in range(2):
                nc.vector.tensor_tensor(
                    st[t][:, halves[h]], s_window[t][:].indirect(n4_t[:, list_halves[h]]),
                    s_plain[t][:, halves[h]], ALU.subtract,
                )

        def take_size(t):
            nc.scalar.activation(size[t][:], st[t][:], ACT.Abs)

        def take_root(t):
            nc.scalar.activation(root[t][:], size[t][:], ACT.Abs_reciprocal_sqrt, bias=0.5)

        def finish(t):
            nc.scalar.activation(inverse[t][:], root[t][:], ACT.Square)
            for h in range(2):
                nc.vector.tensor_tensor(
                    result[h][:, t, :], inverse[t][:].indirect(n5_t[:, list_halves[h]]), st[t][:, halves[h]], ALU.mult
                )
                nc.sync.dma_start(out_rows[:, t, halves[h]], result[h][:, t, :])

        for bank, cols in ((s_first, halves[0]), (s_ps[0], halves[1])):
            leave_by_scalar(s_window[0], bank, cols)
            leave_by_scalar(s_plain[0], bank, cols)
        centre(0)
        leave_by_scalar(s_window[1], s_ps[1], whole)
        leave_by_vector(s_plain[1], s_ps[1], whole)
        centre(1)
        leave_by_scalar(s_window[3], s_ps[3], whole)
        nc.sync.dma_start(s_plain[3][:], s_window[3][:])
        leave_by_scalar(s_window[2], s_ps[2], whole)
        take_size(0)
        leave_by_scalar(s_plain[2], s_ps[2], halves[0])
        leave_by_vector(s_plain[2], s_ps[2], halves[1])
        centre(2)
        centre(3)
        for t in range(PACK):
            take_root(t)
            if t + 1 < PACK:
                take_size(t + 1)
            finish(t)

        out_w = keep.tile([P, N], I32, name="out_w", align_bytes=64)
        out_s = keep.tile([P, N], U8, name="out_s", align_bytes=64)
        words_out = out_1[0].rearrange("p n t -> p (n t)").bitcast(I32)
        for h, regroup in enumerate((nc.scalar.copy, nc.vector.tensor_copy)):
            out_in = keep.tile([P, HALF, PACK], BF16, name=f"out_in{h}", align_bytes=64)
            regroup(
                out_in[:].rearrange("p (c i) t -> p c t i", i=LINE // 4),
                result[h][:].rearrange("p t (c i) -> p c t i", i=LINE // 4),
            )
            nc.vector.quantize_mx(
                out=out_w[:, halves[h]].bitcast(FP8X4), scales=out_s[:, halves[h]],
                in_=out_in[:].rearrange("p c t -> p (c t)"),
            )
            nc.sync.dma_start(words_out[:, halves[h]], out_w[:, halves[h]])
        for q in range(P // QUADRANT):
            queue = nc.sync if q % 2 == 0 else nc.scalar
            queue.dma_start(
                out_2[0, 4 * q : 4 * q + 4, :].bitcast(I32), out_s[QUADRANT * q : QUADRANT * q + 4, :].bitcast(I32)
            )
